import numpy as np
import ml_dtypes


def mxq(x, axis, fmt="e4m3"):
    dtype, down = {"e4m3": (ml_dtypes.float8_e4m3fn, 7), "e5m2": (ml_dtypes.float8_e5m2, 14)}[fmt]
    v = np.moveaxis(np.asarray(x, np.float32).astype(ml_dtypes.bfloat16).astype(np.float64), axis, -1)
    blocks = v.reshape(v.shape[:-1] + (-1, 32))
    amax = np.abs(blocks).max(-1, keepdims=True)
    byte = np.maximum(np.where(amax > 0, np.frexp(amax)[1] - 1 + 127, 0) - down, 1)
    scale = np.exp2(byte - 127.0)
    codes = (blocks / scale).astype(np.float32).astype(dtype).astype(np.float64)
    return np.moveaxis((codes * scale).reshape(v.shape), -1, axis)


WIDE = False


def mx_kscale(k):
    if not WIDE:
        return np.ones(k)
    levels = np.array([30, -30])
    if k % 512:
        return np.exp2(np.random.permutation(np.resize(levels, k // 32))).repeat(32)
    a = np.empty((k // 512, 16))
    for p in range(k // 512):
        a[p, :8] = np.random.permutation(np.resize(levels, 8))
        for g in range(8):
            far = levels[np.abs(levels - a[p, g]) >= 10]
            a[p, g + 8] = far[np.random.randint(len(far))]
    return np.exp2(a.ravel()).repeat(32)


def f64(x):
    return np.asarray(x).astype(np.float64)


def striped(idx):
    return np.tile(np.asarray(idx).reshape(-1, 16).T, (8, 1)).astype(np.uint16)


def unstriped(offs):
    return offs[:16].T.reshape(-1).astype(np.int64)


E2M1 = np.array([0.0, 0.5, 1.0, 1.5, 2.0, 3.0, 4.0, 6.0, -0.0, -0.5, -1.0, -1.5, -2.0, -3.0, -4.0, -6.0])


def pack_weight(w, fmt):
    k, n = w.shape
    w = f64(np.asarray(w, np.float32).astype(ml_dtypes.bfloat16)).reshape(k // 32, 32, n)
    amax = np.abs(w).max(1)
    if fmt in ("e4m3", "e5m2"):
        byte = np.frexp(amax)[1] - 1 + 127 - (7 if fmt == "e4m3" else 14)
    else:
        mant, ex = np.frexp(amax / 6.0)
        byte = np.where(mant > 0.5, ex, ex - 1) + 127
    byte = np.clip(np.where(amax > 0, byte, 1), 1, 254)
    scaled = (w * np.exp2(127.0 - byte)[:, None, :]).reshape(k, n).astype(np.float32)
    by_word = np.ascontiguousarray(scaled.reshape(k // 512, 128, 4, n).transpose(0, 1, 3, 2))
    if fmt in ("e4m3", "e5m2"):
        words = by_word.astype(ml_dtypes.float8_e4m3fn if fmt == "e4m3" else ml_dtypes.float8_e5m2).view(np.uint8)
    else:
        c = by_word.astype(ml_dtypes.float4_e2m1fn).view(np.uint8) & 0xF
        words = (c[..., 0::2] | (c[..., 1::2] << 4)).reshape(k // 512, 128, 2 * n)
    return np.ascontiguousarray(words), np.ascontiguousarray(byte.astype(np.uint8).reshape(k // 512, 16, n))


def unpack_weight(words, scales, fmt):
    g, _, n = scales.shape
    words = np.ascontiguousarray(words).reshape(g, 128, n, -1)
    if fmt in ("e4m3", "e5m2"):
        vals = words.view(ml_dtypes.float8_e4m3fn if fmt == "e4m3" else ml_dtypes.float8_e5m2).astype(np.float64)
    else:
        nib = np.empty((g, 128, n, 4), np.uint8)
        nib[..., 0::2] = words & 0xF
        nib[..., 1::2] = words >> 4
        vals = E2M1[nib]
    vals = vals * np.repeat(np.exp2(scales.astype(np.float64) - 127.0), 8, axis=1)[..., None]
    return vals.transpose(0, 1, 3, 2).reshape(g * 512, n)


def bf(x):
    return np.asarray(x, np.float32).astype(ml_dtypes.bfloat16)


def planes(Y):
    r, m = Y.shape
    b = f64(bf(Y)).reshape(r // 32, 32, m)
    amax = np.abs(b).max(1)
    byte = np.clip(np.where(amax > 0, np.frexp(amax)[1] - 1 + 127 - 7, 1), 1, 254)
    codes = (b * np.exp2(127.0 - byte)[:, None, :]).reshape(r, m).astype(np.float32).astype(ml_dtypes.float8_e4m3fn).view(np.uint8)
    words = codes.reshape(r // 512, 128, 4, m).transpose(0, 1, 3, 2)
    return np.ascontiguousarray(words), np.ascontiguousarray(byte.astype(np.uint8).reshape(r // 512, 16, m))


K, T, J, I, L, S, R, N = 512, 1024, 256, 128, 128, 512, 512, 512


def setup_inputs():
    n = np.random.standard_normal
    idx = np.random.permutation(T)[:I]
    idx2 = np.random.permutation(S)[:L]
    fk = mx_kscale(K)
    fr = mx_kscale(R)
    wp = pack_weight(n((K, R)) * 1 / np.sqrt(K) * fk[:, None] * fr, "e5m2")
    return {
        "xa": (n((K, T)) / fk[:, None]).astype(np.float32),
        "xb": (n((K, S)) * 0.6 / fk[:, None]).astype(np.float32),
        "w_words": wp[0],
        "w_scales": wp[1],
        "wb": (n((R, N)) * 1 / np.sqrt(R) / fr[:, None]).astype(np.float32),
        "rs": (n((N, J))).astype(np.float32),
        "offs": striped(idx),
        "offs2": striped(idx2),
    }


def reference(xa, xb, w_words, w_scales, wb, rs, offs, offs2):
    idx = unstriped(offs)
    idx2 = unstriped(offs2)
    wu = unpack_weight(w_words, w_scales, "e5m2")
    u = np.concatenate([f64(xa)[:, idx], f64(xb)[:, idx2]], axis=1)
    uq = mxq(u, 0, "e4m3")
    a = wu.T @ uq
    hid = np.maximum(a, 0.0)
    wbq = mxq(f64(wb), 0, "e4m3")
    hidq = mxq(hid, 0, "e5m2")
    p = wbq.T @ hidq
    p1 = np.pad(p, ((0, 0), (1, 0)))[:, :J]
    y = p - 0.7 * p1 + 0.5 * f64(rs)
    words, scales = planes(y)
    return y, words, scales

@@ -1,0 +1,200 @@
+from contextlib import ExitStack
+
+import concourse.mybir as mybir
+
+K, T, J, S, R, N = 512, 1024, 256, 512, 512, 512
+FLOPS = 2 * K * R * J + 2 * R * N * J
+
+F32 = mybir.dt.float32
+BF16 = mybir.dt.bfloat16
+I32 = mybir.dt.int32
+U32 = mybir.dt.uint32
+U16 = mybir.dt.uint16
+U8 = mybir.dt.uint8
+E4M3 = mybir.dt.float8_e4m3fn_x4
+E5M2 = mybir.dt.float8_e5m2_x4
+ALU = mybir.AluOpType
+ACT = mybir.ActivationFunctionType
+
+P = 128
+PACK = 4
+HALF = J // 2
+LAG = -0.7
+RES = 0.5
+
+
+def tile_list_joined_plain_lagged_pl_kernel(tc, xa, xb, w_words, w_scales, wb, rs, offs, offs2, out_0, out_1, out_2):
+    nc = tc.nc
+    with ExitStack() as ctx:
+        sb = ctx.enter_context(tc.tile_pool(name="sb", bufs=1))
+        ps = ctx.enter_context(tc.psum_pool(name="ps", bufs=1))
+
+        def tile(shape, dtype, name, tag=None):
+            return sb.tile(shape, dtype, name=name, tag=tag or name, align_bytes=64)
+
+        list_a = sb.tile([P, HALF // 16], U16, name="list_a")
+        list_b = sb.tile([P, HALF // 16], U16, name="list_b")
+        nc.sync.dma_start(list_a[:], offs)
+        nc.sync.dma_start(list_b[:], offs2)
+
+        w_raw = tile([P, R], U32, "w_raw")
+        nc.sync.dma_start(w_raw[:].bitcast(I32), w_words[0].rearrange("p r t -> p (r t)").bitcast(I32))
+        ws_raw = tile([P, R], U8, "ws_raw")
+        nc.gpsimd.memset(ws_raw[:].bitcast(I32), 0)
+        for q in range(4):
+            nc.scalar.dma_start(ws_raw[32 * q : 32 * q + 4, :].bitcast(I32), w_scales[0, 4 * q : 4 * q + 4, :].bitcast(I32))
+
+        xa_rows = xa.rearrange("(p t) c -> p t c", t=PACK)
+        xb_rows = xb.rearrange("(p t) c -> p t c", t=PACK)
+        xa_sb = [tile([P, T], F32, f"xa{t}") for t in range(PACK)]
+        xb_pair = tile([P, 2, S], F32, "xb01")
+        xb_sb = [xb_pair[:, 0, :], xb_pair[:, 1, :], tile([P, S], F32, "xb2")[:], tile([P, S], F32, "xb3")[:]]
+        for t in range(PACK):
+            nc.sync.dma_start(xa_sb[t][:], xa_rows[:, t, :])
+        nc.sync.dma_start(xb_pair[:], xb_rows[:, 0:2, :])
+        for t in (2, 3):
+            nc.sync.dma_start(xb_sb[t], xb_rows[:, t, :])
+
+        wb_rows = wb.rearrange("(p s) n -> p s n", s=PACK)
+        wb_raw = [tile([P, PACK, N // 2], F32, f"wb_raw{h}") for h in range(2)]
+        for h in range(2):
+            nc.sync.dma_start(wb_raw[h][:], wb_rows[:, :, h * (N // 2) : (h + 1) * (N // 2)])
+
+        rs_rows = rs.rearrange("(p t) j -> p t j", t=PACK)
+        rs_sb = [tile([P, 2, J], F32, f"rs{b}") for b in range(2)]
+        for b in range(2):
+            nc.sync.dma_start(rs_sb[b][:], rs_rows[:, 2 * b : 2 * b + 2, :])
+
+        w_codes = tile([P, R], U32, "w_codes")
+        w_plane = tile([P, R], U8, "w_plane")
+        nc.vector.tensor_copy(w_codes[:].rearrange("p (t m) -> p m t", t=PACK), w_raw[:].rearrange("p (m t) -> p m t", t=PACK))
+        nc.vector.tensor_copy(w_plane[:].rearrange("p (t m) -> p m t", t=PACK), ws_raw[:].rearrange("p (m t) -> p m t", t=PACK))
+
+        u_bf = [tile([P, HALF, PACK], BF16, f"u_bf{h}") for h in range(2)]
+        picked = tile([P, 2, HALF], BF16, "picked")
+        for t in (0, 1):
+            nc.scalar.activation(picked[:, t, :], xa_sb[t][:].indirect(list_a[:]), ACT.Copy)
+        nc.scalar.copy(u_bf[0][:, :, 0:2], picked[:].rearrange("p t j -> p j t"))
+        for t in (2, 3):
+            nc.vector.tensor_copy(u_bf[0][:, :, t], xa_sb[t][:].indirect(list_a[:]))
+
+        hid_plane = tile([P, J], U8, "hid_plane")
+
+        hid_bf = [tile([P, HALF, PACK], BF16, f"hid_bf{h}") for h in range(2)]
+
+        def first_product(h):
+            u_codes = tile([P, HALF], U32, f"u_codes{h}")
+            u_plane = tile([P, HALF], U8, f"u_plane{h}")
+            nc.vector.quantize_mx(out=u_codes[:].bitcast(E4M3), scales=u_plane[:], in_=u_bf[h][:].rearrange("p j t -> p (j t)"))
+            acc = ps.tile([P, PACK, HALF], F32, name=f"acc{h}")
+            for t in range(PACK):
+                cols = slice(t * P, (t + 1) * P)
+                nc.tensor.matmul_mx(
+                    out=acc[:, t, :],
+                    lhsT=w_codes[:, cols].bitcast(E5M2),
+                    lhsT_scale=w_plane[:, cols],
+                    rhs=u_codes[:].bitcast(E4M3),
+                    rhs_scale=u_plane[:],
+                    start=True,
+                    stop=True,
+                )
+            return acc
+
+        def relu(h, acc):
+            nc.scalar.activation(hid_bf[h][:], acc[:].rearrange("p t j -> p j t"), ACT.Relu)
+
+        def quantise_hid(h):
+            cols = slice(h * HALF, (h + 1) * HALF)
+            nc.vector.quantize_mx(
+                out=hid_codes[:, cols].bitcast(E5M2), scales=hid_plane[:, cols], in_=hid_bf[h][:].rearrange("p j t -> p (j t)")
+            )
+
+        wb_bf = tile([P, PACK, P, PACK], BF16, "wb_bf")
+
+        def round_wb(h, slices, copy):
+            src = wb_raw[h][:].rearrange("p s (m t) -> p m s t", t=PACK)[:, :, :, slices]
+            copy(wb_bf[:, slices, h * (P // 2) : (h + 1) * (P // 2), :].rearrange("p t m s -> p m s t"), src)
+
+        front_codes = tile([P, 2, P], U32, "front_codes")
+        front_plane = tile([P, 2, P], U8, "front_plane")
+
+        def quantise_front(h):
+            ms = slice(h * (P // 2), (h + 1) * (P // 2))
+            for t in range(2):
+                nc.vector.quantize_mx(
+                    out=front_codes[:, t, ms].bitcast(E4M3),
+                    scales=front_plane[:, t, ms],
+                    in_=wb_bf[:, t, ms, :].rearrange("p m s -> p (m s)"),
+                )
+
+        relu(0, first_product(0))
+        for t in range(PACK):
+            nc.vector.tensor_copy(u_bf[1][:, :, t], xb_sb[t].indirect(list_b[:]))
+        acc_b = first_product(1)
+        hid_codes = tile([P, J], U32, "hid_codes", "u_bf1")
+        quantise_hid(0)
+        round_wb(0, slice(0, 4), nc.vector.tensor_copy)
+        relu(1, acc_b)
+        quantise_front(0)
+        round_wb(1, slice(0, 2), nc.vector.tensor_copy)
+        round_wb(1, slice(2, 4), nc.scalar.copy)
+        quantise_front(1)
+        quantise_hid(1)
+        back_codes = tile([P, 2, P], U32, "back_codes", "hid_bf1")
+        back_plane = tile([P, 2, P], U8, "back_plane")
+        nc.vector.quantize_mx(
+            out=back_codes[:].rearrange("p t m -> p (t m)").bitcast(E4M3),
+            scales=back_plane[:].rearrange("p t m -> p (t m)"),
+            in_=wb_bf[:, 2:4].rearrange("p t m s -> p (t m s)"),
+        )
+
+        prod = [ps.tile([P, 2, J], F32, name=f"prod{b}") for b in range(2)]
+        for b, (codes, plane) in enumerate(((front_codes, front_plane), (back_codes, back_plane))):
+            for e in range(2):
+                nc.tensor.matmul_mx(
+                    out=prod[b][:, e, :],
+                    lhsT=codes[:, e, :].bitcast(E4M3),
+                    lhsT_scale=plane[:, e, :],
+                    rhs=hid_codes[:].bitcast(E5M2),
+                    rhs_scale=hid_plane[:],
+                    start=True,
+                    stop=True,
+                )
+
+        y_codes = tile([P, J], U32, "y_codes")
+        y_plane = tile([P, J], U8, "y_plane")
+        out_rows = out_0.rearrange("(p t) j -> p t j", t=PACK)
+        out_words = out_1[0].rearrange("p c t -> p (c t)").bitcast(I32)
+        for h in range(2):
+            cols = slice(h * HALF, (h + 1) * HALF)
+            skip = 1 if h == 0 else 0
+            y = tile([P, PACK, HALF], F32, f"y{h}")
+            y_bf = tile([P, HALF, PACK], BF16, f"y_bf{h}")
+            pair = [slice(0, 2), slice(2, 4)]
+            before = [prod[b][:, :, h * HALF + skip - 1 : (h + 1) * HALF - 1] for b in range(2)]
+            if h == 0:
+                for b in range(2):
+                    nc.vector.scalar_tensor_tensor(y[:, pair[b], :], rs_sb[b][:, :, cols], RES, prod[b][:, :, cols], ALU.mult, ALU.add)
+                for b in range(2):
+                    nc.vector.scalar_tensor_tensor(y[:, pair[b], skip:], before[b], LAG, y[:, pair[b], skip:], ALU.mult, ALU.add)
+                nc.sync.dma_start(out_rows[:, :, cols], y[:])
+                nc.scalar.copy(y_bf[:], y[:].rearrange("p t j -> p j t"))
+            else:
+                part = tile([P, 2, HALF], F32, "part")
+                nc.vector.scalar_tensor_tensor(y[:, pair[0], :], rs_sb[0][:, :, cols], RES, prod[0][:, :, cols], ALU.mult, ALU.add)
+                nc.vector.scalar_tensor_tensor(part[:], rs_sb[1][:, :, cols], RES, prod[1][:, :, cols], ALU.mult, ALU.add)
+                nc.vector.scalar_tensor_tensor(y[:, pair[0], :], before[0], LAG, y[:, pair[0], :], ALU.mult, ALU.add)
+                nc.sync.dma_start(out_rows[:, pair[0], cols], y[:, pair[0], :])
+                nc.scalar.copy(y_bf[:, :, pair[0]], y[:, pair[0], :].rearrange("p t j -> p j t"))
+                nc.vector.scalar_tensor_tensor(
+                    y_bf[:, :, pair[1]], before[1].rearrange("p t j -> p j t"), LAG, part[:].rearrange("p t j -> p j t"), ALU.mult, ALU.add
+                )
+                nc.vector.scalar_tensor_tensor(y[:, pair[1], :], before[1], LAG, part[:], ALU.mult, ALU.add)
+                nc.sync.dma_start(out_rows[:, pair[1], cols], y[:, pair[1], :])
+            nc.vector.quantize_mx(
+                out=y_codes[:, cols].bitcast(E4M3), scales=y_plane[:, cols], in_=y_bf[:].rearrange("p j t -> p (j t)")
+            )
+            nc.sync.dma_start(out_words[:, cols], y_codes[:, cols].bitcast(I32))
+        for q in range(4):
+            queue = nc.sync if q == 0 else nc.scalar
+            queue.dma_start(out_2[0, 4 * q : 4 * q + 4, :].bitcast(I32), y_plane[32 * q : 32 * q + 4, :].bitcast(I32))

@@ -34,31 +34,30 @@ def tile_list_joined_plain_lagged_pl_kernel(tc, xa, xb, w_words, w_scales, wb, r
 
         list_a = sb.tile([P, HALF // 16], U16, name="list_a")
         list_b = sb.tile([P, HALF // 16], U16, name="list_b")
-        nc.sync.dma_start(list_a[:], offs)
-        nc.sync.dma_start(list_b[:], offs2)
 
         w_raw = tile([P, R], U32, "w_raw")
-        nc.sync.dma_start(w_raw[:].bitcast(I32), w_words[0].rearrange("p r t -> p (r t)").bitcast(I32))
-        ws_raw = tile([P, R], U8, "ws_raw")
-        nc.gpsimd.memset(ws_raw[:].bitcast(I32), 0)
+        ws_in = tile([P, R // 4], I32, "ws_in")
         for q in range(4):
-            nc.scalar.dma_start(ws_raw[32 * q : 32 * q + 4, :].bitcast(I32), w_scales[0, 4 * q : 4 * q + 4, :].bitcast(I32))
+            nc.scalar.dma_start(ws_in[32 * q : 32 * q + 4, :], w_scales[0, 4 * q : 4 * q + 4, :].bitcast(I32))
 
         xa_rows = xa.rearrange("(p t) c -> p t c", t=PACK)
         xb_rows = xb.rearrange("(p t) c -> p t c", t=PACK)
         xa_sb = [tile([P, T], F32, f"xa{t}") for t in range(PACK)]
         xb_pair = tile([P, 2, S], F32, "xb01")
         xb_sb = [xb_pair[:, 0, :], xb_pair[:, 1, :], tile([P, S], F32, "xb2")[:], tile([P, S], F32, "xb3")[:]]
+        nc.sync.dma_start(list_a[:], offs)
+        nc.sync.dma_start(list_b[:], offs2)
         for t in range(PACK):
             nc.sync.dma_start(xa_sb[t][:], xa_rows[:, t, :])
-        nc.sync.dma_start(xb_pair[:], xb_rows[:, 0:2, :])
-        for t in (2, 3):
-            nc.sync.dma_start(xb_sb[t], xb_rows[:, t, :])
-
+            if t == 1:
+                nc.sync.dma_start(w_raw[:].bitcast(I32), w_words[0].rearrange("p r t -> p (r t)").bitcast(I32))
         wb_rows = wb.rearrange("(p s) n -> p s n", s=PACK)
         wb_raw = [tile([P, PACK, N // 2], F32, f"wb_raw{h}") for h in range(2)]
-        for h in range(2):
-            nc.sync.dma_start(wb_raw[h][:], wb_rows[:, :, h * (N // 2) : (h + 1) * (N // 2)])
+        nc.sync.dma_start(xb_pair[:], xb_rows[:, 0:2, :])
+        nc.sync.dma_start(wb_raw[0][:], wb_rows[:, :, : N // 2])
+        for t in (2, 3):
+            nc.sync.dma_start(xb_sb[t], xb_rows[:, t, :])
+        nc.sync.dma_start(wb_raw[1][:], wb_rows[:, :, N // 2 :])
 
         rs_rows = rs.rearrange("(p t) j -> p t j", t=PACK)
         rs_sb = [tile([P, 2, J], F32, f"rs{b}") for b in range(2)]
@@ -67,6 +66,10 @@ def tile_list_joined_plain_lagged_pl_kernel(tc, xa, xb, w_words, w_scales, wb, r
 
         w_codes = tile([P, R], U32, "w_codes")
         w_plane = tile([P, R], U8, "w_plane")
+        ws_raw = tile([P, R], U8, "ws_raw")
+        nc.vector.memset(ws_raw[:].bitcast(I32), 0)
+        for q in range(4):
+            nc.vector.tensor_copy(ws_raw[32 * q : 32 * q + 4, :].bitcast(I32), ws_in[32 * q : 32 * q + 4, :])
         nc.vector.tensor_copy(w_codes[:].rearrange("p (t m) -> p m t", t=PACK), w_raw[:].rearrange("p (m t) -> p m t", t=PACK))
         nc.vector.tensor_copy(w_plane[:].rearrange("p (t m) -> p m t", t=PACK), ws_raw[:].rearrange("p (m t) -> p m t", t=PACK))
 
@@ -78,9 +81,6 @@ def tile_list_joined_plain_lagged_pl_kernel(tc, xa, xb, w_words, w_scales, wb, r
         for t in (2, 3):
             nc.vector.tensor_copy(u_bf[0][:, :, t], xa_sb[t][:].indirect(list_a[:]))
 
-        hid_plane = tile([P, J], U8, "hid_plane")
-
-        hid_bf = [tile([P, HALF, PACK], BF16, f"hid_bf{h}") for h in range(2)]
 
         def first_product(h):
             u_codes = tile([P, HALF], U32, f"u_codes{h}")
@@ -100,63 +100,54 @@ def tile_list_joined_plain_lagged_pl_kernel(tc, xa, xb, w_words, w_scales, wb, r
                 )
             return acc
 
-        def relu(h, acc):
-            nc.scalar.activation(hid_bf[h][:], acc[:].rearrange("p t j -> p j t"), ACT.Relu)
+        def hidden(h, acc, tag):
+            hid_bf = tile([P, HALF, PACK], BF16, f"hid_bf{h}")
+            nc.scalar.activation(hid_bf[:], acc[:].rearrange("p t j -> p j t"), ACT.Relu)
+            codes = tile([P, HALF], U32, f"hid_codes{h}")
+            plane = tile([P, HALF], U8, f"hid_plane{h}", tag)
+            nc.vector.quantize_mx(out=codes[:].bitcast(E5M2), scales=plane[:], in_=hid_bf[:].rearrange("p j t -> p (j t)"))
+            return codes, plane
 
-        def quantise_hid(h):
-            cols = slice(h * HALF, (h + 1) * HALF)
-            nc.vector.quantize_mx(
-                out=hid_codes[:, cols].bitcast(E5M2), scales=hid_plane[:, cols], in_=hid_bf[h][:].rearrange("p j t -> p (j t)")
-            )
+        wb_codes = [tile([P, P], U32, f"wb_codes{t}") for t in range(PACK)]
+        wb_plane = [tile([P, P], U8, f"wb_plane{t}") for t in range(PACK)]
+        wb_bf = [tile([P, PACK, P // 2, PACK], BF16, f"wb_bf{h}") for h in range(2)]
 
-        wb_bf = tile([P, PACK, P, PACK], BF16, "wb_bf")
+        def round_wb(h, ms, copy):
+            copy(wb_bf[h][:].rearrange("p t m s -> p m s t")[:, ms], wb_raw[h][:].rearrange("p s (m t) -> p m s t", t=PACK)[:, ms])
 
-        def round_wb(h, slices, copy):
-            src = wb_raw[h][:].rearrange("p s (m t) -> p m s t", t=PACK)[:, :, :, slices]
-            copy(wb_bf[:, slices, h * (P // 2) : (h + 1) * (P // 2), :].rearrange("p t m s -> p m s t"), src)
-
-        front_codes = tile([P, 2, P], U32, "front_codes")
-        front_plane = tile([P, 2, P], U8, "front_plane")
-
-        def quantise_front(h):
+        def quantise_wb(h):
             ms = slice(h * (P // 2), (h + 1) * (P // 2))
-            for t in range(2):
+            for t in range(PACK):
                 nc.vector.quantize_mx(
-                    out=front_codes[:, t, ms].bitcast(E4M3),
-                    scales=front_plane[:, t, ms],
-                    in_=wb_bf[:, t, ms, :].rearrange("p m s -> p (m s)"),
+                    out=wb_codes[t][:, ms].bitcast(E4M3),
+                    scales=wb_plane[t][:, ms],
+                    in_=wb_bf[h][:, t].rearrange("p m s -> p (m s)"),
                 )
 
-        relu(0, first_product(0))
-        for t in range(PACK):
+        acc_a = first_product(0)
+        for t in (0, 1):
+            nc.vector.tensor_copy(u_bf[1][:, :, t], xb_sb[t].indirect(list_b[:]))
+        round_wb(0, slice(0, P // 2), nc.vector.tensor_copy)
+        quantise_wb(0)
+        for t in (2, 3):
             nc.vector.tensor_copy(u_bf[1][:, :, t], xb_sb[t].indirect(list_b[:]))
         acc_b = first_product(1)
-        hid_codes = tile([P, J], U32, "hid_codes", "u_bf1")
-        quantise_hid(0)
-        round_wb(0, slice(0, 4), nc.vector.tensor_copy)
-        relu(1, acc_b)
-        quantise_front(0)
-        round_wb(1, slice(0, 2), nc.vector.tensor_copy)
-        round_wb(1, slice(2, 4), nc.scalar.copy)
-        quantise_front(1)
-        quantise_hid(1)
-        back_codes = tile([P, 2, P], U32, "back_codes", "hid_bf1")
-        back_plane = tile([P, 2, P], U8, "back_plane")
-        nc.vector.quantize_mx(
-            out=back_codes[:].rearrange("p t m -> p (t m)").bitcast(E4M3),
-            scales=back_plane[:].rearrange("p t m -> p (t m)"),
-            in_=wb_bf[:, 2:4].rearrange("p t m s -> p (t m s)"),
-        )
+        hid = [hidden(0, acc_a, "u_bf1")]
+        round_wb(1, slice(0, P // 2), nc.vector.tensor_copy)
+        quantise_wb(1)
+        hid.append(hidden(1, acc_b, "wb_bf1"))
 
-        prod = [ps.tile([P, 2, J], F32, name=f"prod{b}") for b in range(2)]
-        for b, (codes, plane) in enumerate(((front_codes, front_plane), (back_codes, back_plane))):
-            for e in range(2):
+        halves = [slice(0, HALF), slice(HALF, J)]
+        pairs = [slice(0, 2), slice(2, 4)]
+        prod = [[ps.tile([P, 2, HALF], F32, name=f"prod{h}{b}") for b in range(2)] for h in range(2)]
+        for h in range(2):
+            for t in range(PACK):
                 nc.tensor.matmul_mx(
-                    out=prod[b][:, e, :],
-                    lhsT=codes[:, e, :].bitcast(E4M3),
-                    lhsT_scale=plane[:, e, :],
-                    rhs=hid_codes[:].bitcast(E5M2),
-                    rhs_scale=hid_plane[:],
+                    out=prod[h][t // 2][:, t % 2, :],
+                    lhsT=wb_codes[t][:].bitcast(E4M3),
+                    lhsT_scale=wb_plane[t][:],
+                    rhs=hid[h][0][:].bitcast(E5M2),
+                    rhs_scale=hid[h][1][:],
                     start=True,
                     stop=True,
                 )
@@ -165,36 +156,47 @@ def tile_list_joined_plain_lagged_pl_kernel(tc, xa, xb, w_words, w_scales, wb, r
         y_plane = tile([P, J], U8, "y_plane")
         out_rows = out_0.rearrange("(p t) j -> p t j", t=PACK)
         out_words = out_1[0].rearrange("p c t -> p (c t)").bitcast(I32)
-        for h in range(2):
-            cols = slice(h * HALF, (h + 1) * HALF)
-            skip = 1 if h == 0 else 0
-            y = tile([P, PACK, HALF], F32, f"y{h}")
-            y_bf = tile([P, HALF, PACK], BF16, f"y_bf{h}")
-            pair = [slice(0, 2), slice(2, 4)]
-            before = [prod[b][:, :, h * HALF + skip - 1 : (h + 1) * HALF - 1] for b in range(2)]
-            if h == 0:
-                for b in range(2):
-                    nc.vector.scalar_tensor_tensor(y[:, pair[b], :], rs_sb[b][:, :, cols], RES, prod[b][:, :, cols], ALU.mult, ALU.add)
-                for b in range(2):
-                    nc.vector.scalar_tensor_tensor(y[:, pair[b], skip:], before[b], LAG, y[:, pair[b], skip:], ALU.mult, ALU.add)
-                nc.sync.dma_start(out_rows[:, :, cols], y[:])
-                nc.scalar.copy(y_bf[:], y[:].rearrange("p t j -> p j t"))
-            else:
-                part = tile([P, 2, HALF], F32, "part")
-                nc.vector.scalar_tensor_tensor(y[:, pair[0], :], rs_sb[0][:, :, cols], RES, prod[0][:, :, cols], ALU.mult, ALU.add)
-                nc.vector.scalar_tensor_tensor(part[:], rs_sb[1][:, :, cols], RES, prod[1][:, :, cols], ALU.mult, ALU.add)
-                nc.vector.scalar_tensor_tensor(y[:, pair[0], :], before[0], LAG, y[:, pair[0], :], ALU.mult, ALU.add)
-                nc.sync.dma_start(out_rows[:, pair[0], cols], y[:, pair[0], :])
-                nc.scalar.copy(y_bf[:, :, pair[0]], y[:, pair[0], :].rearrange("p t j -> p j t"))
-                nc.vector.scalar_tensor_tensor(
-                    y_bf[:, :, pair[1]], before[1].rearrange("p t j -> p j t"), LAG, part[:].rearrange("p t j -> p j t"), ALU.mult, ALU.add
-                )
-                nc.vector.scalar_tensor_tensor(y[:, pair[1], :], before[1], LAG, part[:], ALU.mult, ALU.add)
-                nc.sync.dma_start(out_rows[:, pair[1], cols], y[:, pair[1], :])
+        y = [tile([P, PACK, HALF], F32, f"y{h}") for h in range(2)]
+        y_bf = [tile([P, HALF, PACK], BF16, f"y_bf{h}") for h in range(2)]
+
+        def take_lag(h, b):
+            first = h * HALF + 1
+            count = min(HALF, J - first)
+            dst = rs_sb[b][:, :, first : first + count]
+            nc.vector.scalar_tensor_tensor(dst, prod[h][b][:, :, :count], LAG / RES, dst, ALU.mult, ALU.add)
+
+        def finish(h, b):
+            nc.vector.scalar_tensor_tensor(y[h][:, pairs[b], :], rs_sb[b][:, :, halves[h]], RES, prod[h][b][:], ALU.mult, ALU.add)
+
+        def quantise_y(h):
             nc.vector.quantize_mx(
-                out=y_codes[:, cols].bitcast(E4M3), scales=y_plane[:, cols], in_=y_bf[:].rearrange("p j t -> p (j t)")
+                out=y_codes[:, halves[h]].bitcast(E4M3), scales=y_plane[:, halves[h]], in_=y_bf[h][:].rearrange("p j t -> p (j t)")
             )
-            nc.sync.dma_start(out_words[:, cols], y_codes[:, cols].bitcast(I32))
+            nc.sync.dma_start(out_words[:, halves[h]], y_codes[:, halves[h]].bitcast(I32))
+
+        for b in range(2):
+            take_lag(0, b)
+        for b in range(2):
+            finish(0, b)
+        nc.sync.dma_start(out_rows[:, :, halves[0]], y[0][:])
+        nc.scalar.copy(y_bf[0][:], y[0][:].rearrange("p t j -> p j t"))
+        for b in range(2):
+            take_lag(1, b)
+        finish(1, 0)
+        nc.sync.dma_start(out_rows[:, pairs[0], halves[1]], y[1][:, pairs[0], :])
+        nc.scalar.copy(y_bf[1][:, :, pairs[0]], y[1][:, pairs[0], :].rearrange("p t j -> p j t"))
+        quantise_y(0)
+        nc.vector.scalar_tensor_tensor(
+            y_bf[1][:, :, pairs[1]],
+            rs_sb[1][:, :, halves[1]].rearrange("p t j -> p j t"),
+            RES,
+            prod[1][1][:].rearrange("p t j -> p j t"),
+            ALU.mult,
+            ALU.add,
+        )
+        finish(1, 1)
+        nc.sync.dma_start(out_rows[:, pairs[1], halves[1]], y[1][:, pairs[1], :])
+        quantise_y(1)
         for q in range(4):
-            queue = nc.sync if q == 0 else nc.scalar
+            queue = nc.sync if q < 2 else nc.scalar
             queue.dma_start(out_2[0, 4 * q : 4 * q + 4, :].bitcast(I32), y_plane[32 * q : 32 * q + 4, :].bitcast(I32))

from contextlib import ExitStack

import concourse.mybir as mybir

K, T, J, S, R, N = 512, 1024, 256, 512, 512, 512
FLOPS = 2 * K * R * J + 2 * R * N * J

F32 = mybir.dt.float32
BF16 = mybir.dt.bfloat16
I32 = mybir.dt.int32
U32 = mybir.dt.uint32
U16 = mybir.dt.uint16
U8 = mybir.dt.uint8
E4M3 = mybir.dt.float8_e4m3fn_x4
E5M2 = mybir.dt.float8_e5m2_x4
ALU = mybir.AluOpType
ACT = mybir.ActivationFunctionType

P = 128
PACK = 4
HALF = J // 2
LAG = -0.7
RES = 0.5


def tile_list_joined_plain_lagged_pl_kernel(tc, xa, xb, w_words, w_scales, wb, rs, offs, offs2, out_0, out_1, out_2):
    nc = tc.nc
    with ExitStack() as ctx:
        sb = ctx.enter_context(tc.tile_pool(name="sb", bufs=1))
        ps = ctx.enter_context(tc.psum_pool(name="ps", bufs=1))

        def tile(shape, dtype, name, tag=None):
            return sb.tile(shape, dtype, name=name, tag=tag or name, align_bytes=64)

        list_a = sb.tile([P, HALF // 16], U16, name="list_a")
        list_b = sb.tile([P, HALF // 16], U16, name="list_b")

        w_raw = tile([P, R], U32, "w_raw")
        ws_in = tile([P, R // 4], I32, "ws_in")
        for q in range(4):
            nc.scalar.dma_start(ws_in[32 * q : 32 * q + 4, :], w_scales[0, 4 * q : 4 * q + 4, :].bitcast(I32))

        xa_rows = xa.rearrange("(p t) c -> p t c", t=PACK)
        xb_rows = xb.rearrange("(p t) c -> p t c", t=PACK)
        xa_sb = [tile([P, T], F32, f"xa{t}") for t in range(PACK)]
        xb_pair = tile([P, 2, S], F32, "xb01")
        xb_sb = [xb_pair[:, 0, :], xb_pair[:, 1, :], tile([P, S], F32, "xb2")[:], tile([P, S], F32, "xb3")[:]]
        nc.sync.dma_start(list_a[:], offs)
        nc.sync.dma_start(list_b[:], offs2)
        for t in range(PACK):
            nc.sync.dma_start(xa_sb[t][:], xa_rows[:, t, :])
            if t == 1:
                nc.sync.dma_start(w_raw[:].bitcast(I32), w_words[0].rearrange("p r t -> p (r t)").bitcast(I32))
        wb_rows = wb.rearrange("(p s) n -> p s n", s=PACK)
        wb_raw = [tile([P, PACK, N // 2], F32, f"wb_raw{h}") for h in range(2)]
        nc.sync.dma_start(xb_pair[:], xb_rows[:, 0:2, :])
        nc.sync.dma_start(wb_raw[0][:], wb_rows[:, :, : N // 2])
        for t in (2, 3):
            nc.sync.dma_start(xb_sb[t], xb_rows[:, t, :])
        nc.sync.dma_start(wb_raw[1][:], wb_rows[:, :, N // 2 :])

        rs_rows = rs.rearrange("(p t) j -> p t j", t=PACK)
        rs_sb = [tile([P, 2, J], F32, f"rs{b}") for b in range(2)]
        for b in range(2):
            nc.sync.dma_start(rs_sb[b][:], rs_rows[:, 2 * b : 2 * b + 2, :])

        w_codes = tile([P, R], U32, "w_codes")
        w_plane = tile([P, R], U8, "w_plane")
        ws_raw = tile([P, R], U8, "ws_raw")
        nc.vector.memset(ws_raw[:].bitcast(I32), 0)
        for q in range(4):
            nc.vector.tensor_copy(ws_raw[32 * q : 32 * q + 4, :].bitcast(I32), ws_in[32 * q : 32 * q + 4, :])
        nc.vector.tensor_copy(w_codes[:].rearrange("p (t m) -> p m t", t=PACK), w_raw[:].rearrange("p (m t) -> p m t", t=PACK))
        nc.vector.tensor_copy(w_plane[:].rearrange("p (t m) -> p m t", t=PACK), ws_raw[:].rearrange("p (m t) -> p m t", t=PACK))

        u_bf = [tile([P, HALF, PACK], BF16, f"u_bf{h}") for h in range(2)]
        picked = tile([P, 2, HALF], BF16, "picked")
        for t in (0, 1):
            nc.scalar.activation(picked[:, t, :], xa_sb[t][:].indirect(list_a[:]), ACT.Copy)
        nc.scalar.copy(u_bf[0][:, :, 0:2], picked[:].rearrange("p t j -> p j t"))
        for t in (2, 3):
            nc.vector.tensor_copy(u_bf[0][:, :, t], xa_sb[t][:].indirect(list_a[:]))


        def first_product(h):
            u_codes = tile([P, HALF], U32, f"u_codes{h}")
            u_plane = tile([P, HALF], U8, f"u_plane{h}")
            nc.vector.quantize_mx(out=u_codes[:].bitcast(E4M3), scales=u_plane[:], in_=u_bf[h][:].rearrange("p j t -> p (j t)"))
            acc = ps.tile([P, PACK, HALF], F32, name=f"acc{h}")
            for t in range(PACK):
                cols = slice(t * P, (t + 1) * P)
                nc.tensor.matmul_mx(
                    out=acc[:, t, :],
                    lhsT=w_codes[:, cols].bitcast(E5M2),
                    lhsT_scale=w_plane[:, cols],
                    rhs=u_codes[:].bitcast(E4M3),
                    rhs_scale=u_plane[:],
                    start=True,
                    stop=True,
                )
            return acc

        def hidden(h, acc, tag):
            hid_bf = tile([P, HALF, PACK], BF16, f"hid_bf{h}")
            nc.scalar.activation(hid_bf[:], acc[:].rearrange("p t j -> p j t"), ACT.Relu)
            codes = tile([P, HALF], U32, f"hid_codes{h}")
            plane = tile([P, HALF], U8, f"hid_plane{h}", tag)
            nc.vector.quantize_mx(out=codes[:].bitcast(E5M2), scales=plane[:], in_=hid_bf[:].rearrange("p j t -> p (j t)"))
            return codes, plane

        wb_codes = [tile([P, P], U32, f"wb_codes{t}") for t in range(PACK)]
        wb_plane = [tile([P, P], U8, f"wb_plane{t}") for t in range(PACK)]
        wb_bf = [tile([P, PACK, P // 2, PACK], BF16, f"wb_bf{h}") for h in range(2)]

        def round_wb(h, ms, copy):
            copy(wb_bf[h][:].rearrange("p t m s -> p m s t")[:, ms], wb_raw[h][:].rearrange("p s (m t) -> p m s t", t=PACK)[:, ms])

        def quantise_wb(h):
            ms = slice(h * (P // 2), (h + 1) * (P // 2))
            for t in range(PACK):
                nc.vector.quantize_mx(
                    out=wb_codes[t][:, ms].bitcast(E4M3),
                    scales=wb_plane[t][:, ms],
                    in_=wb_bf[h][:, t].rearrange("p m s -> p (m s)"),
                )

        acc_a = first_product(0)
        for t in (0, 1):
            nc.vector.tensor_copy(u_bf[1][:, :, t], xb_sb[t].indirect(list_b[:]))
        round_wb(0, slice(0, P // 2), nc.vector.tensor_copy)
        quantise_wb(0)
        for t in (2, 3):
            nc.vector.tensor_copy(u_bf[1][:, :, t], xb_sb[t].indirect(list_b[:]))
        acc_b = first_product(1)
        hid = [hidden(0, acc_a, "u_bf1")]
        round_wb(1, slice(0, P // 2), nc.vector.tensor_copy)
        quantise_wb(1)
        hid.append(hidden(1, acc_b, "wb_bf1"))

        halves = [slice(0, HALF), slice(HALF, J)]
        pairs = [slice(0, 2), slice(2, 4)]
        prod = [[ps.tile([P, 2, HALF], F32, name=f"prod{h}{b}") for b in range(2)] for h in range(2)]
        for h in range(2):
            for t in range(PACK):
                nc.tensor.matmul_mx(
                    out=prod[h][t // 2][:, t % 2, :],
                    lhsT=wb_codes[t][:].bitcast(E4M3),
                    lhsT_scale=wb_plane[t][:],
                    rhs=hid[h][0][:].bitcast(E5M2),
                    rhs_scale=hid[h][1][:],
                    start=True,
                    stop=True,
                )

        y_codes = tile([P, J], U32, "y_codes")
        y_plane = tile([P, J], U8, "y_plane")
        out_rows = out_0.rearrange("(p t) j -> p t j", t=PACK)
        out_words = out_1[0].rearrange("p c t -> p (c t)").bitcast(I32)
        y = [tile([P, PACK, HALF], F32, f"y{h}") for h in range(2)]
        y_bf = [tile([P, HALF, PACK], BF16, f"y_bf{h}") for h in range(2)]

        def take_lag(h, b):
            first = h * HALF + 1
            count = min(HALF, J - first)
            dst = rs_sb[b][:, :, first : first + count]
            nc.vector.scalar_tensor_tensor(dst, prod[h][b][:, :, :count], LAG / RES, dst, ALU.mult, ALU.add)

        def finish(h, b):
            nc.vector.scalar_tensor_tensor(y[h][:, pairs[b], :], rs_sb[b][:, :, halves[h]], RES, prod[h][b][:], ALU.mult, ALU.add)

        def quantise_y(h):
            nc.vector.quantize_mx(
                out=y_codes[:, halves[h]].bitcast(E4M3), scales=y_plane[:, halves[h]], in_=y_bf[h][:].rearrange("p j t -> p (j t)")
            )
            nc.sync.dma_start(out_words[:, halves[h]], y_codes[:, halves[h]].bitcast(I32))

        for b in range(2):
            take_lag(0, b)
        for b in range(2):
            finish(0, b)
        nc.sync.dma_start(out_rows[:, :, halves[0]], y[0][:])
        nc.scalar.copy(y_bf[0][:], y[0][:].rearrange("p t j -> p j t"))
        for b in range(2):
            take_lag(1, b)
        finish(1, 0)
        nc.sync.dma_start(out_rows[:, pairs[0], halves[1]], y[1][:, pairs[0], :])
        nc.scalar.copy(y_bf[1][:, :, pairs[0]], y[1][:, pairs[0], :].rearrange("p t j -> p j t"))
        quantise_y(0)
        nc.vector.scalar_tensor_tensor(
            y_bf[1][:, :, pairs[1]],
            rs_sb[1][:, :, halves[1]].rearrange("p t j -> p j t"),
            RES,
            prod[1][1][:].rearrange("p t j -> p j t"),
            ALU.mult,
            ALU.add,
        )
        finish(1, 1)
        nc.sync.dma_start(out_rows[:, pairs[1], halves[1]], y[1][:, pairs[1], :])
        quantise_y(1)
        for q in range(4):
            queue = nc.sync if q < 2 else nc.scalar
            queue.dma_start(out_2[0, 4 * q : 4 * q + 4, :].bitcast(I32), y_plane[32 * q : 32 * q + 4, :].bitcast(I32))
